import numpy as np
import ml_dtypes


def mxq(x, axis, fmt="e4m3"):
    dtype, down = {"e4m3": (ml_dtypes.float8_e4m3fn, 7), "e5m2": (ml_dtypes.float8_e5m2, 14)}[fmt]
    v = np.moveaxis(np.asarray(x, np.float32).astype(ml_dtypes.bfloat16).astype(np.float64), axis, -1)
    blocks = v.reshape(v.shape[:-1] + (-1, 32))
    amax = np.abs(blocks).max(-1, keepdims=True)
    byte = np.maximum(np.where(amax > 0, np.frexp(amax)[1] - 1 + 127, 0) - down, 1)
    scale = np.exp2(byte - 127.0)
    codes = (blocks / scale).astype(np.float32).astype(dtype).astype(np.float64)
    return np.moveaxis((codes * scale).reshape(v.shape), -1, axis)


WIDE = False


def mx_kscale(k):
    if not WIDE:
        return np.ones(k)
    levels = np.array([10, -10, 5, -5, 0])
    if k % 512:
        return np.exp2(np.random.permutation(np.resize(levels, k // 32))).repeat(32)
    a = np.empty((k // 512, 16))
    for p in range(k // 512):
        a[p, :8] = np.random.permutation(np.resize(levels, 8))
        for g in range(8):
            far = levels[np.abs(levels - a[p, g]) >= 10]
            a[p, g + 8] = far[np.random.randint(len(far))]
    return np.exp2(a.ravel()).repeat(32)


BF16 = ml_dtypes.bfloat16


def bf(x):
    return np.asarray(x, np.float32).astype(BF16)


def f64(x):
    return np.asarray(x).astype(np.float64)


E2M1 = np.array([0.0, 0.5, 1.0, 1.5, 2.0, 3.0, 4.0, 6.0, -0.0, -0.5, -1.0, -1.5, -2.0, -3.0, -4.0, -6.0])


def pack_weight(w, fmt):
    k, n = w.shape
    w = f64(bf(w)).reshape(k // 32, 32, n)
    amax = np.abs(w).max(1)
    if fmt == "e4m3":
        byte = np.frexp(amax)[1] - 1 + 127 - 7
    else:
        mant, ex = np.frexp(amax / 6.0)
        byte = np.where(mant > 0.5, ex, ex - 1) + 127
    byte = np.clip(np.where(amax > 0, byte, 1), 1, 254)
    scaled = (w * np.exp2(127.0 - byte)[:, None, :]).reshape(k, n).astype(np.float32)
    by_word = np.ascontiguousarray(scaled.reshape(k // 512, 128, 4, n).transpose(0, 1, 3, 2))
    if fmt == "e4m3":
        words = by_word.astype(ml_dtypes.float8_e4m3fn).view(np.uint8)
    else:
        c = by_word.astype(ml_dtypes.float4_e2m1fn).view(np.uint8) & 0xF
        words = c[..., 0::2] | (c[..., 1::2] << 4)
    return np.ascontiguousarray(words), np.ascontiguousarray(byte.astype(np.uint8).reshape(k // 512, 16, n))


def unpack_weight(words, scales, fmt):
    g, p, n, _ = words.shape
    if fmt == "e4m3":
        vals = np.ascontiguousarray(words).view(ml_dtypes.float8_e4m3fn).astype(np.float64)
    else:
        nib = np.empty((g, p, n, 4), np.uint8)
        nib[..., 0::2] = words & 0xF
        nib[..., 1::2] = words >> 4
        vals = E2M1[nib]
    vals = vals * np.repeat(np.exp2(scales.astype(np.float64) - 127.0), 8, axis=1)[..., None]
    return vals.transpose(0, 1, 3, 2).reshape(g * 512, n)
def pack4(w):
    words, scales = pack_weight(w, "e2m1")
    return words.reshape(words.shape[0], 128, -1), scales


def unpack4(words, scales):
    return unpack_weight(words.reshape(words.shape[0], 128, -1, 2), scales, "e2m1")


def planes(Y):
    n, m = Y.shape
    b = f64(bf(Y)).reshape(n // 32, 32, m)
    amax = np.abs(b).max(1)
    byte = np.clip(np.where(amax > 0, np.frexp(amax)[1] - 1 + 127 - 7, 1), 1, 254)
    codes = (b * np.exp2(127.0 - byte)[:, None, :]).reshape(n, m).astype(np.float32).astype(ml_dtypes.float8_e4m3fn).view(np.uint8)
    words = codes.reshape(n // 512, 128, 4, m).transpose(0, 1, 3, 2)
    return np.ascontiguousarray(words), np.ascontiguousarray(byte.astype(np.uint8).reshape(n // 512, 16, m))


T, K, F = 1024, 1024, 4096

GELU_A = 0.7978845608028654
GELU_B = 0.044715


def setup_inputs():
    s = mx_kscale(K)
    x = np.random.randn(K, T) * s[:, None]
    x_words, x_scales = pack_weight(x, "e4m3")
    w_up = np.random.randn(K, F) / np.sqrt(K) / s[:, None]
    b_up = 0.4 * np.random.randn(F)
    gain = np.exp(0.8 * np.random.randn(F))
    return {"x_words": x_words, "x_scales": x_scales, "w_up": bf(w_up), "b_up": bf(b_up), "gain": bf(gain)}


def reference(x_words, x_scales, w_up, b_up, gain):
    X = unpack_weight(x_words, x_scales, "e4m3")
    Wq = mxq(f64(w_up), 0, "e4m3")
    z = (X.T @ Wq) + f64(b_up)
    h = 0.5 * z * (1.0 + np.tanh(GELU_A * (z + GELU_B * z * z * z)))
    y = h * f64(gain)
    Y = y.T
    words, scales = planes(Y)
    return y, words, scales

@@ -1,0 +1,224 @@
+from contextlib import ExitStack
+
+import concourse.mybir as mybir
+from concourse.masks import make_identity
+
+T, K, F = 1024, 1024, 4096
+FLOPS = 2 * T * K * F
+
+F32 = mybir.dt.float32
+BF16 = mybir.dt.bfloat16
+I32 = mybir.dt.int32
+U32 = mybir.dt.uint32
+U8 = mybir.dt.uint8
+FP8X4 = mybir.dt.float8_e4m3fn_x4
+GELU = mybir.ActivationFunctionType.Gelu_apprx_tanh
+MULT = mybir.AluOpType.mult
+
+P = 128
+PACK = 4
+SPAN = P * PACK
+PASSES = K // SPAN
+GROUPS = F // SPAN
+HALVES = T // SPAN
+UNITS = GROUPS * HALVES
+LINES = SPAN // 8
+HEAD_SPLIT = 40
+SKIP_EVERY = 4
+
+
+def tile_ffn_up_gelu_gain_g6_kernel(tc, x_words, x_scales, w_up, b_up, gain, out_0, out_1, out_2):
+    nc = tc.nc
+    with ExitStack() as ctx:
+        keep = ctx.enter_context(tc.tile_pool(name="keep", bufs=1))
+        work = ctx.enter_context(tc.tile_pool(name="work", bufs=2))
+        psum = ctx.enter_context(tc.psum_pool(name="psum", bufs=1))
+        ctx.enter_context(tc.manual_schedule())
+
+        ident = keep.tile([P, P], F32, name="ident")
+        make_identity(nc, ident[:])
+
+        x_plane = keep.tile([P, T], U8, name="x_plane", align_bytes=64)
+        nc.vector.memset(x_plane[:].bitcast(U32), 0)
+        warm_in = keep.tile([P, 1], F32, name="warm_in")
+        warm_out = keep.tile([P, 1], F32, name="warm_out")
+        nc.vector.memset(warm_in[:], 0.0)
+        nc.scalar.activation(out=warm_out[:], in_=warm_in[:], func=GELU)
+
+        w_raw, x_codes = {}, {}
+
+        def load_w(g, c):
+            raw = keep.tile([P, PACK, SPAN], BF16, name="w_raw_%d_%d" % (g, c))
+            rows = w_up[c * SPAN:(c + 1) * SPAN, g * SPAN:(g + 1) * SPAN]
+            nc.sync.dma_start(out=raw[:], in_=rows.rearrange("(p j) f -> p j f", j=PACK))
+            w_raw[g, c] = raw
+
+        def load_x(c, h):
+            codes = keep.tile([P, SPAN], U32, name="x_codes_%d_%d" % (c, h), align_bytes=64)
+            src = x_words[c].rearrange("p n t -> p (n t)")[:, h * SPAN * PACK:(h + 1) * SPAN * PACK]
+            nc.sync.dma_start(out=codes[:].bitcast(I32), in_=src.bitcast(I32))
+            x_codes[c, h] = codes
+
+        def load_per_unit_vector(vec, name):
+            sb = keep.tile([P, GROUPS * PACK], BF16, name=name)
+            nc.sync.dma_start(out=sb[:].rearrange("p (g t) -> p g t", t=PACK),
+                              in_=vec.rearrange("(g p t) -> p g t", p=P, t=PACK))
+            return sb
+
+        load_w(0, 0)
+        load_w(0, 1)
+        for q in range(4):
+            nc.sync.dma_start(out=x_plane[32 * q:32 * q + 4 * PASSES, :].bitcast(I32),
+                              in_=x_scales[:, 4 * q:4 * q + 4, :].bitcast(I32))
+        load_x(0, 0)
+        load_x(1, 0)
+        bias_sb = load_per_unit_vector(b_up, "bias_sb")
+        load_w(1, 0)
+        gain_sb = load_per_unit_vector(gain, "gain_sb")
+        load_x(0, 1)
+        load_x(1, 1)
+        load_w(1, 1)
+        for g in range(2, GROUPS):
+            for c in range(PASSES):
+                load_w(g, c)
+
+        y_planes = []
+        for i in range(GROUPS // 4):
+            plane = keep.tile([P, T], U8, name="y_plane_%d" % i, align_bytes=64)
+            y_planes.append(plane)
+
+        w_quant, z_bank, h_sb, y_t, y_bank = {}, {}, {}, {}, {}
+        pending = []
+
+        def interleave_w(g, c, split=LINES):
+            grouped = work.tile([P, PACK * SPAN], BF16, name="w_grouped", align_bytes=64)
+            dst = grouped[:].rearrange("p (t a i j) -> p a t i j", t=PACK, i=2, j=PACK)
+            src = w_raw[g, c][:].rearrange("p j (a i t) -> p a t i j", i=2, t=PACK)
+            nc.vector.tensor_copy(out=dst[:, :split], in_=src[:, :split])
+            if split < LINES:
+                nc.scalar.copy(out=dst[:, split:], in_=src[:, split:])
+
+            def quantize():
+                codes = work.tile([P, SPAN], U32, name="w_codes", bufs=6, align_bytes=64)
+                scales = work.tile([P, SPAN], U8, name="w_scales", bufs=6, align_bytes=64)
+                nc.vector.quantize_mx(out=codes[:].bitcast(FP8X4), scales=scales[:], in_=grouped[:])
+                w_quant[g, c] = (codes, scales)
+
+            pending.append(quantize)
+
+        def interleave_y(u):
+            g, h = divmod(u, HALVES)
+            grouped = work.tile([P, PACK * SPAN], BF16, name="y_grouped", align_bytes=64)
+            nc.vector.tensor_copy(out=grouped[:].rearrange("p (c i t) -> p c t i", i=4, t=PACK),
+                                  in_=y_t[u][:].rearrange("p t (c i) -> p c t i", i=4))
+
+            def quantize():
+                codes = work.tile([P, SPAN], U32, name="y_codes", bufs=4, align_bytes=64)
+                plane = y_planes[g // 4]
+                nc.vector.quantize_mx(out=codes[:].bitcast(FP8X4),
+                                      scales=plane[4 * (g % 4):P, h * SPAN:(h + 1) * SPAN], in_=grouped[:])
+                dst = out_1[g].rearrange("p m t -> p (m t)")[:, h * SPAN * PACK:(h + 1) * SPAN * PACK]
+                nc.sync.dma_start(out=dst.bitcast(I32), in_=codes[:].bitcast(I32))
+                if g % 4 == 3 and h == HALVES - 1:
+                    for q in range(4):
+                        nc.sync.dma_start(out=out_2[g - 3:g + 1, 4 * q:4 * q + 4, :].bitcast(I32),
+                                          in_=plane[32 * q:32 * q + 16, :].bitcast(I32))
+
+            pending.append(quantize)
+
+        def flush():
+            for quantize in pending:
+                quantize()
+            pending.clear()
+
+        def multiply(u, pair):
+            g, h = divmod(u, HALVES)
+            for t in (2 * pair, 2 * pair + 1):
+                bank = psum.tile([P, SPAN], F32, name="z_%d" % t)
+                for c in range(PASSES):
+                    codes, scales = w_quant[g, c]
+                    nc.tensor.matmul_mx(out=bank[:],
+                                        lhsT=codes[:, t * P:(t + 1) * P].bitcast(FP8X4),
+                                        lhsT_scale=scales[:, t * P:(t + 1) * P],
+                                        rhs=x_codes[c, h][:].bitcast(FP8X4),
+                                        rhs_scale=x_plane[4 * c:P, h * SPAN:(h + 1) * SPAN],
+                                        start=(c == 0), stop=(c == PASSES - 1))
+                z_bank[u, t] = bank
+
+        def activate(u, pair):
+            g = u // HALVES
+            for t in (2 * pair, 2 * pair + 1):
+                h_tile = work.tile([P, SPAN], F32, name="h_tile", bufs=8)
+                col = g * PACK + t
+                nc.scalar.activation(out=h_tile[:], in_=z_bank[u, t][:], func=GELU, bias=bias_sb[:, col:col + 1])
+                h_sb[u, t] = h_tile
+
+        def apply_gain(u, pair):
+            g = u // HALVES
+            if pair == 0:
+                y_tile = work.tile([P, PACK, SPAN], F32, name="y_tile", bufs=6)
+                y_t[u] = y_tile
+            for t in (2 * pair, 2 * pair + 1):
+                col = g * PACK + t
+                nc.vector.tensor_scalar(out=y_t[u][:, t, :], in0=h_sb[u, t][:], scalar1=gain_sb[:, col:col + 1],
+                                        scalar2=None, op0=MULT)
+
+        def turn(u, pair):
+            for j in (2 * pair, 2 * pair + 1):
+                bank = psum.tile([P, SPAN], F32, name="y_%d" % j)
+                for t in range(PACK):
+                    nc.tensor.transpose(bank[:, t * P:(t + 1) * P], y_t[u][:, t, j * P:(j + 1) * P], ident[:])
+                y_bank[u, j] = bank
+
+        def store_y(u, pair):
+            g, h = divmod(u, HALVES)
+            rows = work.tile([P, 2, SPAN], F32, name="y_rows", bufs=5)
+            for jj in range(2):
+                nc.scalar.copy(out=rows[:, jj, :].rearrange("p (m t) -> p m t", t=PACK),
+                               in_=y_bank[u, 2 * pair + jj][:].rearrange("p (t m) -> p m t", t=PACK))
+            t0 = h * SPAN + pair * 2 * P
+            dst = out_0[t0:t0 + 2 * P, g * SPAN:(g + 1) * SPAN].rearrange("(j p) f -> p j f", p=P)
+            nc.sync.dma_start(out=dst, in_=rows[:])
+
+        for c in range(PASSES):
+            interleave_w(0, c, HEAD_SPLIT)
+        flush()
+        interleave_w(1, 0)
+        multiply(0, 0)
+        multiply(0, 1)
+
+        w_jobs = [(g, c) for g in range(1, GROUPS) for c in range(PASSES)][1:]
+        next_y = 0
+        for u in range(UNITS + 2):
+            live = u < UNITS
+            if live:
+                activate(u, 0)
+                apply_gain(u, 0)
+                flush()
+                if u < len(w_jobs):
+                    interleave_w(*w_jobs[u])
+                else:
+                    interleave_y(next_y)
+                    next_y = next_y + 1
+            if 1 <= u <= UNITS:
+                turn(u - 1, 0)
+            if u + 1 < UNITS:
+                multiply(u + 1, 0)
+            if u >= 2:
+                store_y(u - 2, 1)
+            if live:
+                activate(u, 1)
+                apply_gain(u, 1)
+                flush()
+                if u >= len(w_jobs) or u % SKIP_EVERY != 1:
+                    interleave_y(next_y)
+                    next_y = next_y + 1
+            if u == UNITS - 1:
+                flush()
+            if 1 <= u <= UNITS:
+                turn(u - 1, 1)
+            if u + 1 < UNITS:
+                multiply(u + 1, 1)
+            if 1 <= u <= UNITS:
+                store_y(u - 1, 0)
+        assert next_y == UNITS

@@ -75,9 +75,9 @@ def tile_ffn_up_gelu_gain_g6_kernel(tc, x_words, x_scales, w_up, b_up, gain, out
         bias_sb = load_per_unit_vector(b_up, "bias_sb")
         load_w(1, 0)
         gain_sb = load_per_unit_vector(gain, "gain_sb")
+        load_w(1, 1)
         load_x(0, 1)
         load_x(1, 1)
-        load_w(1, 1)
         for g in range(2, GROUPS):
             for c in range(PASSES):
                 load_w(g, c)
@@ -88,12 +88,12 @@ def tile_ffn_up_gelu_gain_g6_kernel(tc, x_words, x_scales, w_up, b_up, gain, out
             y_planes.append(plane)
 
         w_quant, z_bank, h_sb, y_t, y_bank = {}, {}, {}, {}, {}
-        pending = []
+        pending, plane_stores = [], []
 
         def interleave_w(g, c, split=LINES):
             grouped = work.tile([P, PACK * SPAN], BF16, name="w_grouped", align_bytes=64)
-            dst = grouped[:].rearrange("p (t a i j) -> p a t i j", t=PACK, i=2, j=PACK)
-            src = w_raw[g, c][:].rearrange("p j (a i t) -> p a t i j", i=2, t=PACK)
+            dst = grouped[:].rearrange("p (t a i j) -> p a t j i", t=PACK, i=2, j=PACK)
+            src = w_raw[g, c][:].rearrange("p j (a i t) -> p a t j i", i=2, t=PACK)
             nc.vector.tensor_copy(out=dst[:, :split], in_=src[:, :split])
             if split < LINES:
                 nc.scalar.copy(out=dst[:, split:], in_=src[:, split:])
@@ -109,8 +109,8 @@ def tile_ffn_up_gelu_gain_g6_kernel(tc, x_words, x_scales, w_up, b_up, gain, out
         def interleave_y(u):
             g, h = divmod(u, HALVES)
             grouped = work.tile([P, PACK * SPAN], BF16, name="y_grouped", align_bytes=64)
-            nc.vector.tensor_copy(out=grouped[:].rearrange("p (c i t) -> p c t i", i=4, t=PACK),
-                                  in_=y_t[u][:].rearrange("p t (c i) -> p c t i", i=4))
+            nc.vector.tensor_copy(out=grouped[:].rearrange("p (c i t) -> p c t i", i=2, t=PACK),
+                                  in_=y_t[u][:].rearrange("p t (c i) -> p c t i", i=2))
 
             def quantize():
                 codes = work.tile([P, SPAN], U32, name="y_codes", bufs=4, align_bytes=64)
@@ -118,11 +118,11 @@ def tile_ffn_up_gelu_gain_g6_kernel(tc, x_words, x_scales, w_up, b_up, gain, out
                 nc.vector.quantize_mx(out=codes[:].bitcast(FP8X4),
                                       scales=plane[4 * (g % 4):P, h * SPAN:(h + 1) * SPAN], in_=grouped[:])
                 dst = out_1[g].rearrange("p m t -> p (m t)")[:, h * SPAN * PACK:(h + 1) * SPAN * PACK]
-                nc.sync.dma_start(out=dst.bitcast(I32), in_=codes[:].bitcast(I32))
+                plane_stores.append((dst.bitcast(I32), codes[:].bitcast(I32)))
                 if g % 4 == 3 and h == HALVES - 1:
                     for q in range(4):
-                        nc.sync.dma_start(out=out_2[g - 3:g + 1, 4 * q:4 * q + 4, :].bitcast(I32),
-                                          in_=plane[32 * q:32 * q + 16, :].bitcast(I32))
+                        plane_stores.append((out_2[g - 3:g + 1, 4 * q:4 * q + 4, :].bitcast(I32),
+                                             plane[32 * q:32 * q + 16, :].bitcast(I32)))
 
             pending.append(quantize)
 
@@ -130,6 +130,11 @@ def tile_ffn_up_gelu_gain_g6_kernel(tc, x_words, x_scales, w_up, b_up, gain, out
             for quantize in pending:
                 quantize()
             pending.clear()
+
+        def store_planes():
+            for dst, src in plane_stores:
+                nc.sync.dma_start(out=dst, in_=src)
+            plane_stores.clear()
 
         def multiply(u, pair):
             g, h = divmod(u, HALVES)
@@ -170,55 +175,55 @@ def tile_ffn_up_gelu_gain_g6_kernel(tc, x_words, x_scales, w_up, b_up, gain, out
                     nc.tensor.transpose(bank[:, t * P:(t + 1) * P], y_t[u][:, t, j * P:(j + 1) * P], ident[:])
                 y_bank[u, j] = bank
 
-        def store_y(u, pair):
+        def store_y(u, pair, pieces=1):
             g, h = divmod(u, HALVES)
             rows = work.tile([P, 2, SPAN], F32, name="y_rows", bufs=5)
+            t0 = h * SPAN + pair * 2 * P
+            dst = out_0[t0:t0 + 2 * P, g * SPAN:(g + 1) * SPAN].rearrange("(j p) f -> p j f", p=P)
             for jj in range(2):
                 nc.scalar.copy(out=rows[:, jj, :].rearrange("p (m t) -> p m t", t=PACK),
                                in_=y_bank[u, 2 * pair + jj][:].rearrange("p (t m) -> p m t", t=PACK))
-            t0 = h * SPAN + pair * 2 * P
-            dst = out_0[t0:t0 + 2 * P, g * SPAN:(g + 1) * SPAN].rearrange("(j p) f -> p j f", p=P)
-            nc.sync.dma_start(out=dst, in_=rows[:])
+                if pieces == 2:
+                    nc.sync.dma_start(out=dst[:, jj, :], in_=rows[:, jj, :])
+            if pieces == 1:
+                nc.sync.dma_start(out=dst, in_=rows[:])
 
         for c in range(PASSES):
             interleave_w(0, c, HEAD_SPLIT)
         flush()
-        interleave_w(1, 0)
+        for c in range(PASSES):
+            interleave_w(1, c)
+        flush()
         multiply(0, 0)
         multiply(0, 1)
 
-        w_jobs = [(g, c) for g in range(1, GROUPS) for c in range(PASSES)][1:]
+        w_jobs = [(g, c) for g in range(2, GROUPS) for c in range(PASSES)]
+        steps = 2 * UNITS
         next_y = 0
-        for u in range(UNITS + 2):
-            live = u < UNITS
-            if live:
-                activate(u, 0)
-                apply_gain(u, 0)
-                flush()
-                if u < len(w_jobs):
-                    interleave_w(*w_jobs[u])
-                else:
-                    interleave_y(next_y)
-                    next_y = next_y + 1
-            if 1 <= u <= UNITS:
-                turn(u - 1, 0)
+        for step in range(steps):
+            u, pair = divmod(step, 2)
+            activate(u, pair)
+            apply_gain(u, pair)
+            flush()
+            if pair == 0 and u <= len(w_jobs):
+                if u >= 1:
+                    interleave_w(*w_jobs[u - 1])
+            elif u > len(w_jobs) or u % SKIP_EVERY != 1:
+                interleave_y(next_y)
+                next_y = next_y + 1
+            if step >= 2:
+                turn(u - 1, pair)
             if u + 1 < UNITS:
-                multiply(u + 1, 0)
-            if u >= 2:
-                store_y(u - 2, 1)
-            if live:
-                activate(u, 1)
-                apply_gain(u, 1)
-                flush()
-                if u >= len(w_jobs) or u % SKIP_EVERY != 1:
-                    interleave_y(next_y)
-                    next_y = next_y + 1
-            if u == UNITS - 1:
-                flush()
-            if 1 <= u <= UNITS:
-                turn(u - 1, 1)
-            if u + 1 < UNITS:
-                multiply(u + 1, 1)
-            if 1 <= u <= UNITS:
-                store_y(u - 1, 0)
+                multiply(u + 1, pair)
+            if 3 <= step < steps - 1:
+                store_y(*divmod(step - 3, 2))
+            if step >= steps - 2:
+                store_y(*divmod(step - 2, 2))
+            store_planes()
         assert next_y == UNITS
+        flush()
+        turn(UNITS - 1, 0)
+        store_y(UNITS - 1, 0)
+        store_planes()
+        turn(UNITS - 1, 1)
+        store_y(UNITS - 1, 1, 2)

@@ -22,9 +22,22 @@ PASSES = K // SPAN
 GROUPS = F // SPAN
 HALVES = T // SPAN
 UNITS = GROUPS * HALVES
-LINES = SPAN // 8
-HEAD_SPLIT = 40
-SKIP_EVERY = 4
+STEPS = 2 * UNITS
+QUADRANTS = 4
+ROWS = 4
+PLANES_PER_TILE = 4
+RUNS = SPAN // 8
+
+FIRST_GROUP_SPLIT = 40
+REST_EVERY = 5
+STORE_LAG = 3
+FINE_STORES = 3
+
+W_QUANT_BUFS = 3 * PASSES
+GELU_BUFS = 2 * PACK
+Y_T_BUFS = 6
+Y_CODES_BUFS = 4
+Y_ROWS_BUFS = 5
 
 
 def tile_ffn_up_gelu_gain_g6_kernel(tc, x_words, x_scales, w_up, b_up, gain, out_0, out_1, out_2):
@@ -40,190 +53,204 @@ def tile_ffn_up_gelu_gain_g6_kernel(tc, x_words, x_scales, w_up, b_up, gain, out
 
         x_plane = keep.tile([P, T], U8, name="x_plane", align_bytes=64)
         nc.vector.memset(x_plane[:].bitcast(U32), 0)
-        warm_in = keep.tile([P, 1], F32, name="warm_in")
-        warm_out = keep.tile([P, 1], F32, name="warm_out")
-        nc.vector.memset(warm_in[:], 0.0)
-        nc.scalar.activation(out=warm_out[:], in_=warm_in[:], func=GELU)
+
+        vec_rows = keep.tile([P, SPAN], BF16, name="vec_rows")
+        nc.vector.memset(vec_rows[:], 0.0)
+        for i, vec in enumerate((b_up, gain)):
+            nc.gpsimd.dma_start(out=vec_rows[i * GROUPS:(i + 1) * GROUPS, :], in_=vec.rearrange("(g f) -> g f", f=SPAN))
 
         w_raw, x_codes = {}, {}
 
         def load_w(g, c):
             raw = keep.tile([P, PACK, SPAN], BF16, name="w_raw_%d_%d" % (g, c))
-            rows = w_up[c * SPAN:(c + 1) * SPAN, g * SPAN:(g + 1) * SPAN]
-            nc.sync.dma_start(out=raw[:], in_=rows.rearrange("(p j) f -> p j f", j=PACK))
+            block = w_up[c * SPAN:(c + 1) * SPAN, g * SPAN:(g + 1) * SPAN]
+            nc.sync.dma_start(out=raw[:], in_=block.rearrange("(p j) n -> p j n", j=PACK))
             w_raw[g, c] = raw
 
         def load_x(c, h):
             codes = keep.tile([P, SPAN], U32, name="x_codes_%d_%d" % (c, h), align_bytes=64)
-            src = x_words[c].rearrange("p n t -> p (n t)")[:, h * SPAN * PACK:(h + 1) * SPAN * PACK]
-            nc.sync.dma_start(out=codes[:].bitcast(I32), in_=src.bitcast(I32))
+            words = x_words[c].rearrange("p n t -> p (n t)")[:, h * SPAN * PACK:(h + 1) * SPAN * PACK]
+            nc.sync.dma_start(out=codes[:].bitcast(I32), in_=words.bitcast(I32))
             x_codes[c, h] = codes
 
-        def load_per_unit_vector(vec, name):
-            sb = keep.tile([P, GROUPS * PACK], BF16, name=name)
-            nc.sync.dma_start(out=sb[:].rearrange("p (g t) -> p g t", t=PACK),
-                              in_=vec.rearrange("(g p t) -> p g t", p=P, t=PACK))
-            return sb
-
-        load_w(0, 0)
-        load_w(0, 1)
-        for q in range(4):
-            nc.sync.dma_start(out=x_plane[32 * q:32 * q + 4 * PASSES, :].bitcast(I32),
-                              in_=x_scales[:, 4 * q:4 * q + 4, :].bitcast(I32))
-        load_x(0, 0)
-        load_x(1, 0)
-        bias_sb = load_per_unit_vector(b_up, "bias_sb")
-        load_w(1, 0)
-        gain_sb = load_per_unit_vector(gain, "gain_sb")
-        load_w(1, 1)
-        load_x(0, 1)
-        load_x(1, 1)
+        for c in range(PASSES):
+            load_w(0, c)
+        for c in range(PASSES):
+            load_x(c, 0)
+        for q in range(QUADRANTS):
+            nc.sync.dma_start(out=x_plane[32 * q:32 * q + ROWS * PASSES, :].bitcast(I32),
+                              in_=x_scales[:, ROWS * q:ROWS * (q + 1), :].bitcast(I32))
+        for c in range(PASSES):
+            load_w(1, c)
+        for c in range(PASSES):
+            load_x(c, 1)
         for g in range(2, GROUPS):
             for c in range(PASSES):
                 load_w(g, c)
 
+        vec_bank = psum.tile([P, SPAN], F32, name="y_bank_0")
+        vec_pairs = vec_rows[:].bitcast(F32)
+        for i in range(2):
+            nc.tensor.transpose(vec_bank[:, i * P:(i + 1) * P], vec_pairs[:, i::2], ident[:])
+        vec_cols = keep.tile([P, 2 * GROUPS * PACK], BF16, name="vec_cols")
+
         y_planes = []
-        for i in range(GROUPS // 4):
-            plane = keep.tile([P, T], U8, name="y_plane_%d" % i, align_bytes=64)
-            y_planes.append(plane)
+        for i in range(GROUPS // PLANES_PER_TILE):
+            y_plane = keep.tile([P, T], U8, name="y_plane_%d" % i, align_bytes=64)
+            y_planes.append(y_plane)
 
-        w_quant, z_bank, h_sb, y_t, y_bank = {}, {}, {}, {}, {}
-        pending, plane_stores = [], []
+        w_grouped, w_quant, z_banks, gelus, y_t, y_grouped, y_banks = {}, {}, {}, {}, {}, {}, {}
+        plane_stores = []
 
-        def interleave_w(g, c, split=LINES):
+        def regroup_w(g, c, split=RUNS):
             grouped = work.tile([P, PACK * SPAN], BF16, name="w_grouped", align_bytes=64)
             dst = grouped[:].rearrange("p (t a i j) -> p a t j i", t=PACK, i=2, j=PACK)
             src = w_raw[g, c][:].rearrange("p j (a i t) -> p a t j i", i=2, t=PACK)
             nc.vector.tensor_copy(out=dst[:, :split], in_=src[:, :split])
-            if split < LINES:
+            if split < RUNS:
                 nc.scalar.copy(out=dst[:, split:], in_=src[:, split:])
+            w_grouped[g, c] = grouped
 
-            def quantize():
-                codes = work.tile([P, SPAN], U32, name="w_codes", bufs=6, align_bytes=64)
-                scales = work.tile([P, SPAN], U8, name="w_scales", bufs=6, align_bytes=64)
-                nc.vector.quantize_mx(out=codes[:].bitcast(FP8X4), scales=scales[:], in_=grouped[:])
+        def quantize_w(g, c, first_slot=0, slots=PACK):
+            if first_slot == 0:
+                codes = work.tile([P, SPAN], U32, name="w_codes", bufs=W_QUANT_BUFS, align_bytes=64)
+                scales = work.tile([P, SPAN], U8, name="w_scales", bufs=W_QUANT_BUFS, align_bytes=64)
                 w_quant[g, c] = (codes, scales)
+            codes, scales = w_quant[g, c]
+            lo, hi = first_slot * P, (first_slot + slots) * P
+            nc.vector.quantize_mx(out=codes[:, lo:hi].bitcast(FP8X4), scales=scales[:, lo:hi],
+                                  in_=w_grouped[g, c][:, lo * PACK:hi * PACK])
 
-            pending.append(quantize)
-
-        def interleave_y(u):
-            g, h = divmod(u, HALVES)
+        def regroup_y(u):
             grouped = work.tile([P, PACK * SPAN], BF16, name="y_grouped", align_bytes=64)
-            nc.vector.tensor_copy(out=grouped[:].rearrange("p (c i t) -> p c t i", i=2, t=PACK),
-                                  in_=y_t[u][:].rearrange("p t (c i) -> p c t i", i=2))
+            nc.vector.tensor_copy(out=grouped[:].rearrange("p (a i t) -> p a t i", i=2, t=PACK),
+                                  in_=y_t[u][:].rearrange("p t (a i) -> p a t i", i=2))
+            y_grouped[u] = grouped
 
-            def quantize():
-                codes = work.tile([P, SPAN], U32, name="y_codes", bufs=4, align_bytes=64)
-                plane = y_planes[g // 4]
-                nc.vector.quantize_mx(out=codes[:].bitcast(FP8X4),
-                                      scales=plane[4 * (g % 4):P, h * SPAN:(h + 1) * SPAN], in_=grouped[:])
-                dst = out_1[g].rearrange("p m t -> p (m t)")[:, h * SPAN * PACK:(h + 1) * SPAN * PACK]
-                plane_stores.append((dst.bitcast(I32), codes[:].bitcast(I32)))
-                if g % 4 == 3 and h == HALVES - 1:
-                    for q in range(4):
-                        plane_stores.append((out_2[g - 3:g + 1, 4 * q:4 * q + 4, :].bitcast(I32),
-                                             plane[32 * q:32 * q + 16, :].bitcast(I32)))
-
-            pending.append(quantize)
-
-        def flush():
-            for quantize in pending:
-                quantize()
-            pending.clear()
+        def quantize_y(u):
+            g, h = divmod(u, HALVES)
+            codes = work.tile([P, SPAN], U32, name="y_codes", bufs=Y_CODES_BUFS, align_bytes=64)
+            tile_index, place = divmod(g, PLANES_PER_TILE)
+            plane = y_planes[tile_index]
+            nc.vector.quantize_mx(out=codes[:].bitcast(FP8X4), scales=plane[ROWS * place:P, h * SPAN:(h + 1) * SPAN],
+                                  in_=y_grouped[u][:])
+            words = out_1[g].rearrange("p m t -> p (m t)")[:, h * SPAN * PACK:(h + 1) * SPAN * PACK]
+            plane_stores.append((words.bitcast(I32), codes[:].bitcast(I32)))
+            if place == PLANES_PER_TILE - 1 and h == HALVES - 1:
+                for q in range(QUADRANTS):
+                    rows = out_2[g - place:g + 1, ROWS * q:ROWS * (q + 1), :]
+                    live = plane[32 * q:32 * q + ROWS * PLANES_PER_TILE, :]
+                    plane_stores.append((rows.bitcast(I32), live.bitcast(I32)))
 
         def store_planes():
             for dst, src in plane_stores:
                 nc.sync.dma_start(out=dst, in_=src)
             plane_stores.clear()
 
-        def multiply(u, pair):
+        def multiply(step):
+            u, pair = divmod(step, 2)
             g, h = divmod(u, HALVES)
             for t in (2 * pair, 2 * pair + 1):
-                bank = psum.tile([P, SPAN], F32, name="z_%d" % t)
+                bank = psum.tile([P, SPAN], F32, name="z_bank_%d" % t)
                 for c in range(PASSES):
                     codes, scales = w_quant[g, c]
                     nc.tensor.matmul_mx(out=bank[:],
                                         lhsT=codes[:, t * P:(t + 1) * P].bitcast(FP8X4),
                                         lhsT_scale=scales[:, t * P:(t + 1) * P],
                                         rhs=x_codes[c, h][:].bitcast(FP8X4),
-                                        rhs_scale=x_plane[4 * c:P, h * SPAN:(h + 1) * SPAN],
+                                        rhs_scale=x_plane[ROWS * c:P, h * SPAN:(h + 1) * SPAN],
                                         start=(c == 0), stop=(c == PASSES - 1))
-                z_bank[u, t] = bank
+                z_banks[u, t] = bank
 
-        def activate(u, pair):
-            g = u // HALVES
+        def activate(step):
+            u, pair = divmod(step, 2)
             for t in (2 * pair, 2 * pair + 1):
-                h_tile = work.tile([P, SPAN], F32, name="h_tile", bufs=8)
-                col = g * PACK + t
-                nc.scalar.activation(out=h_tile[:], in_=z_bank[u, t][:], func=GELU, bias=bias_sb[:, col:col + 1])
-                h_sb[u, t] = h_tile
+                gelu = work.tile([P, SPAN], F32, name="gelu", bufs=GELU_BUFS)
+                col = (u // HALVES) * PACK + t
+                nc.scalar.activation(out=gelu[:], in_=z_banks[u, t][:], func=GELU, bias=vec_cols[:, col:col + 1])
+                gelus[u, t] = gelu
 
-        def apply_gain(u, pair):
-            g = u // HALVES
+        def apply_gain(step):
+            u, pair = divmod(step, 2)
             if pair == 0:
-                y_tile = work.tile([P, PACK, SPAN], F32, name="y_tile", bufs=6)
-                y_t[u] = y_tile
+                y_unit = work.tile([P, PACK, SPAN], F32, name="y_unit", bufs=Y_T_BUFS)
+                y_t[u] = y_unit
             for t in (2 * pair, 2 * pair + 1):
-                col = g * PACK + t
-                nc.vector.tensor_scalar(out=y_t[u][:, t, :], in0=h_sb[u, t][:], scalar1=gain_sb[:, col:col + 1],
+                col = (GROUPS + u // HALVES) * PACK + t
+                nc.vector.tensor_scalar(out=y_t[u][:, t, :], in0=gelus[u, t][:], scalar1=vec_cols[:, col:col + 1],
                                         scalar2=None, op0=MULT)
 
-        def turn(u, pair):
+        def turn(step):
+            u, pair = divmod(step, 2)
             for j in (2 * pair, 2 * pair + 1):
-                bank = psum.tile([P, SPAN], F32, name="y_%d" % j)
+                bank = psum.tile([P, SPAN], F32, name="y_bank_%d" % j)
                 for t in range(PACK):
                     nc.tensor.transpose(bank[:, t * P:(t + 1) * P], y_t[u][:, t, j * P:(j + 1) * P], ident[:])
-                y_bank[u, j] = bank
+                y_banks[u, j] = bank
 
-        def store_y(u, pair, pieces=1):
+        def store_y(step):
+            u, pair = divmod(step, 2)
             g, h = divmod(u, HALVES)
-            rows = work.tile([P, 2, SPAN], F32, name="y_rows", bufs=5)
-            t0 = h * SPAN + pair * 2 * P
-            dst = out_0[t0:t0 + 2 * P, g * SPAN:(g + 1) * SPAN].rearrange("(j p) f -> p j f", p=P)
-            for jj in range(2):
-                nc.scalar.copy(out=rows[:, jj, :].rearrange("p (m t) -> p m t", t=PACK),
-                               in_=y_bank[u, 2 * pair + jj][:].rearrange("p (t m) -> p m t", t=PACK))
-                if pieces == 2:
-                    nc.sync.dma_start(out=dst[:, jj, :], in_=rows[:, jj, :])
-            if pieces == 1:
-                nc.sync.dma_start(out=dst, in_=rows[:])
+            fine = step >= STEPS - FINE_STORES
+            y_rows = work.tile([P, 2, SPAN], F32, name="y_rows", bufs=Y_ROWS_BUFS)
+            first = h * SPAN + pair * 2 * P
+            dst = out_0[first:first + 2 * P, g * SPAN:(g + 1) * SPAN].rearrange("(i p) f -> p i f", p=P)
+            for i in range(2):
+                nc.scalar.copy(out=y_rows[:, i, :].rearrange("p (m t) -> p m t", t=PACK),
+                               in_=y_banks[u, 2 * pair + i][:].rearrange("p (t m) -> p m t", t=PACK))
+                if fine:
+                    nc.sync.dma_start(out=dst[:, i, :], in_=y_rows[:, i, :])
+            if not fine:
+                nc.sync.dma_start(out=dst, in_=y_rows[:])
 
         for c in range(PASSES):
-            interleave_w(0, c, HEAD_SPLIT)
-        flush()
+            regroup_w(0, c, FIRST_GROUP_SPLIT)
+        for first_slot in (0, 2):
+            for c in range(PASSES):
+                quantize_w(0, c, first_slot, 2)
+        nc.vector.tensor_copy(out=vec_cols[:].bitcast(F32).rearrange("p (r i) -> p r i", i=2),
+                              in_=vec_bank[:, :2 * P].rearrange("p (i r) -> p r i", i=2)[:, :2 * GROUPS, :])
         for c in range(PASSES):
-            interleave_w(1, c)
-        flush()
-        multiply(0, 0)
-        multiply(0, 1)
+            regroup_w(1, c)
+        for c in range(PASSES):
+            quantize_w(1, c)
+        multiply(0)
+        multiply(1)
 
         w_jobs = [(g, c) for g in range(2, GROUPS) for c in range(PASSES)]
-        steps = 2 * UNITS
         next_y = 0
-        for step in range(steps):
+        waiting = None
+        for step in range(STEPS):
             u, pair = divmod(step, 2)
-            activate(u, pair)
-            apply_gain(u, pair)
-            flush()
-            if pair == 0 and u <= len(w_jobs):
-                if u >= 1:
-                    interleave_w(*w_jobs[u - 1])
-            elif u > len(w_jobs) or u % SKIP_EVERY != 1:
-                interleave_y(next_y)
+            activate(step)
+            apply_gain(step)
+            if waiting is not None:
+                waiting[0](*waiting[1])
+                waiting = None
+            rest = pair == 1 and u <= len(w_jobs) and u % REST_EVERY == 0
+            if pair == 0 and 1 <= u <= len(w_jobs):
+                regroup_w(*w_jobs[u - 1])
+                waiting = (quantize_w, w_jobs[u - 1])
+            elif not rest and step not in (0, STEPS - 2):
+                regroup_y(next_y)
+                waiting = (quantize_y, (next_y,))
                 next_y = next_y + 1
             if step >= 2:
-                turn(u - 1, pair)
-            if u + 1 < UNITS:
-                multiply(u + 1, pair)
-            if 3 <= step < steps - 1:
-                store_y(*divmod(step - 3, 2))
-            if step >= steps - 2:
-                store_y(*divmod(step - 2, 2))
+                turn(step - 2)
+            if step + 2 < STEPS:
+                multiply(step + 2)
+            if STORE_LAG <= step < STEPS - 1:
+                store_y(step - STORE_LAG)
+            if step >= STEPS - 2:
+                store_y(step - STORE_LAG + 1)
             store_planes()
-        assert next_y == UNITS
-        flush()
-        turn(UNITS - 1, 0)
-        store_y(UNITS - 1, 0)
+
+        assert next_y == UNITS - 1
+        regroup_y(UNITS - 1)
+        quantize_y(UNITS - 2)
+        quantize_y(UNITS - 1)
+        for step in (STEPS - 2, STEPS - 1):
+            turn(step)
+        for step in (STEPS - 2, STEPS - 1):
+            store_y(step)
         store_planes()
-        turn(UNITS - 1, 1)
-        store_y(UNITS - 1, 1, 2)

from contextlib import ExitStack

import concourse.mybir as mybir
from concourse.masks import make_identity

T, K, F = 1024, 1024, 4096
FLOPS = 2 * T * K * F

F32 = mybir.dt.float32
BF16 = mybir.dt.bfloat16
I32 = mybir.dt.int32
U32 = mybir.dt.uint32
U8 = mybir.dt.uint8
FP8X4 = mybir.dt.float8_e4m3fn_x4
GELU = mybir.ActivationFunctionType.Gelu_apprx_tanh
MULT = mybir.AluOpType.mult

P = 128
PACK = 4
SPAN = P * PACK
PASSES = K // SPAN
GROUPS = F // SPAN
HALVES = T // SPAN
UNITS = GROUPS * HALVES
STEPS = 2 * UNITS
QUADRANTS = 4
ROWS = 4
PLANES_PER_TILE = 4
RUNS = SPAN // 8

FIRST_GROUP_SPLIT = 40
REST_EVERY = 5
STORE_LAG = 3
FINE_STORES = 3

W_QUANT_BUFS = 3 * PASSES
GELU_BUFS = 2 * PACK
Y_T_BUFS = 6
Y_CODES_BUFS = 4
Y_ROWS_BUFS = 5


def tile_ffn_up_gelu_gain_g6_kernel(tc, x_words, x_scales, w_up, b_up, gain, out_0, out_1, out_2):
    nc = tc.nc
    with ExitStack() as ctx:
        keep = ctx.enter_context(tc.tile_pool(name="keep", bufs=1))
        work = ctx.enter_context(tc.tile_pool(name="work", bufs=2))
        psum = ctx.enter_context(tc.psum_pool(name="psum", bufs=1))
        ctx.enter_context(tc.manual_schedule())

        ident = keep.tile([P, P], F32, name="ident")
        make_identity(nc, ident[:])

        x_plane = keep.tile([P, T], U8, name="x_plane", align_bytes=64)
        nc.vector.memset(x_plane[:].bitcast(U32), 0)

        vec_rows = keep.tile([P, SPAN], BF16, name="vec_rows")
        nc.vector.memset(vec_rows[:], 0.0)
        for i, vec in enumerate((b_up, gain)):
            nc.gpsimd.dma_start(out=vec_rows[i * GROUPS:(i + 1) * GROUPS, :], in_=vec.rearrange("(g f) -> g f", f=SPAN))

        w_raw, x_codes = {}, {}

        def load_w(g, c):
            raw = keep.tile([P, PACK, SPAN], BF16, name="w_raw_%d_%d" % (g, c))
            block = w_up[c * SPAN:(c + 1) * SPAN, g * SPAN:(g + 1) * SPAN]
            nc.sync.dma_start(out=raw[:], in_=block.rearrange("(p j) n -> p j n", j=PACK))
            w_raw[g, c] = raw

        def load_x(c, h):
            codes = keep.tile([P, SPAN], U32, name="x_codes_%d_%d" % (c, h), align_bytes=64)
            words = x_words[c].rearrange("p n t -> p (n t)")[:, h * SPAN * PACK:(h + 1) * SPAN * PACK]
            nc.sync.dma_start(out=codes[:].bitcast(I32), in_=words.bitcast(I32))
            x_codes[c, h] = codes

        for c in range(PASSES):
            load_w(0, c)
        for c in range(PASSES):
            load_x(c, 0)
        for q in range(QUADRANTS):
            nc.sync.dma_start(out=x_plane[32 * q:32 * q + ROWS * PASSES, :].bitcast(I32),
                              in_=x_scales[:, ROWS * q:ROWS * (q + 1), :].bitcast(I32))
        for c in range(PASSES):
            load_w(1, c)
        for c in range(PASSES):
            load_x(c, 1)
        for g in range(2, GROUPS):
            for c in range(PASSES):
                load_w(g, c)

        vec_bank = psum.tile([P, SPAN], F32, name="y_bank_0")
        vec_pairs = vec_rows[:].bitcast(F32)
        for i in range(2):
            nc.tensor.transpose(vec_bank[:, i * P:(i + 1) * P], vec_pairs[:, i::2], ident[:])
        vec_cols = keep.tile([P, 2 * GROUPS * PACK], BF16, name="vec_cols")

        y_planes = []
        for i in range(GROUPS // PLANES_PER_TILE):
            y_plane = keep.tile([P, T], U8, name="y_plane_%d" % i, align_bytes=64)
            y_planes.append(y_plane)

        w_grouped, w_quant, z_banks, gelus, y_t, y_grouped, y_banks = {}, {}, {}, {}, {}, {}, {}
        plane_stores = []

        def regroup_w(g, c, split=RUNS):
            grouped = work.tile([P, PACK * SPAN], BF16, name="w_grouped", align_bytes=64)
            dst = grouped[:].rearrange("p (t a i j) -> p a t j i", t=PACK, i=2, j=PACK)
            src = w_raw[g, c][:].rearrange("p j (a i t) -> p a t j i", i=2, t=PACK)
            nc.vector.tensor_copy(out=dst[:, :split], in_=src[:, :split])
            if split < RUNS:
                nc.scalar.copy(out=dst[:, split:], in_=src[:, split:])
            w_grouped[g, c] = grouped

        def quantize_w(g, c, first_slot=0, slots=PACK):
            if first_slot == 0:
                codes = work.tile([P, SPAN], U32, name="w_codes", bufs=W_QUANT_BUFS, align_bytes=64)
                scales = work.tile([P, SPAN], U8, name="w_scales", bufs=W_QUANT_BUFS, align_bytes=64)
                w_quant[g, c] = (codes, scales)
            codes, scales = w_quant[g, c]
            lo, hi = first_slot * P, (first_slot + slots) * P
            nc.vector.quantize_mx(out=codes[:, lo:hi].bitcast(FP8X4), scales=scales[:, lo:hi],
                                  in_=w_grouped[g, c][:, lo * PACK:hi * PACK])

        def regroup_y(u):
            grouped = work.tile([P, PACK * SPAN], BF16, name="y_grouped", align_bytes=64)
            nc.vector.tensor_copy(out=grouped[:].rearrange("p (a i t) -> p a t i", i=2, t=PACK),
                                  in_=y_t[u][:].rearrange("p t (a i) -> p a t i", i=2))
            y_grouped[u] = grouped

        def quantize_y(u):
            g, h = divmod(u, HALVES)
            codes = work.tile([P, SPAN], U32, name="y_codes", bufs=Y_CODES_BUFS, align_bytes=64)
            tile_index, place = divmod(g, PLANES_PER_TILE)
            plane = y_planes[tile_index]
            nc.vector.quantize_mx(out=codes[:].bitcast(FP8X4), scales=plane[ROWS * place:P, h * SPAN:(h + 1) * SPAN],
                                  in_=y_grouped[u][:])
            words = out_1[g].rearrange("p m t -> p (m t)")[:, h * SPAN * PACK:(h + 1) * SPAN * PACK]
            plane_stores.append((words.bitcast(I32), codes[:].bitcast(I32)))
            if place == PLANES_PER_TILE - 1 and h == HALVES - 1:
                for q in range(QUADRANTS):
                    rows = out_2[g - place:g + 1, ROWS * q:ROWS * (q + 1), :]
                    live = plane[32 * q:32 * q + ROWS * PLANES_PER_TILE, :]
                    plane_stores.append((rows.bitcast(I32), live.bitcast(I32)))

        def store_planes():
            for dst, src in plane_stores:
                nc.sync.dma_start(out=dst, in_=src)
            plane_stores.clear()

        def multiply(step):
            u, pair = divmod(step, 2)
            g, h = divmod(u, HALVES)
            for t in (2 * pair, 2 * pair + 1):
                bank = psum.tile([P, SPAN], F32, name="z_bank_%d" % t)
                for c in range(PASSES):
                    codes, scales = w_quant[g, c]
                    nc.tensor.matmul_mx(out=bank[:],
                                        lhsT=codes[:, t * P:(t + 1) * P].bitcast(FP8X4),
                                        lhsT_scale=scales[:, t * P:(t + 1) * P],
                                        rhs=x_codes[c, h][:].bitcast(FP8X4),
                                        rhs_scale=x_plane[ROWS * c:P, h * SPAN:(h + 1) * SPAN],
                                        start=(c == 0), stop=(c == PASSES - 1))
                z_banks[u, t] = bank

        def activate(step):
            u, pair = divmod(step, 2)
            for t in (2 * pair, 2 * pair + 1):
                gelu = work.tile([P, SPAN], F32, name="gelu", bufs=GELU_BUFS)
                col = (u // HALVES) * PACK + t
                nc.scalar.activation(out=gelu[:], in_=z_banks[u, t][:], func=GELU, bias=vec_cols[:, col:col + 1])
                gelus[u, t] = gelu

        def apply_gain(step):
            u, pair = divmod(step, 2)
            if pair == 0:
                y_unit = work.tile([P, PACK, SPAN], F32, name="y_unit", bufs=Y_T_BUFS)
                y_t[u] = y_unit
            for t in (2 * pair, 2 * pair + 1):
                col = (GROUPS + u // HALVES) * PACK + t
                nc.vector.tensor_scalar(out=y_t[u][:, t, :], in0=gelus[u, t][:], scalar1=vec_cols[:, col:col + 1],
                                        scalar2=None, op0=MULT)

        def turn(step):
            u, pair = divmod(step, 2)
            for j in (2 * pair, 2 * pair + 1):
                bank = psum.tile([P, SPAN], F32, name="y_bank_%d" % j)
                for t in range(PACK):
                    nc.tensor.transpose(bank[:, t * P:(t + 1) * P], y_t[u][:, t, j * P:(j + 1) * P], ident[:])
                y_banks[u, j] = bank

        def store_y(step):
            u, pair = divmod(step, 2)
            g, h = divmod(u, HALVES)
            fine = step >= STEPS - FINE_STORES
            y_rows = work.tile([P, 2, SPAN], F32, name="y_rows", bufs=Y_ROWS_BUFS)
            first = h * SPAN + pair * 2 * P
            dst = out_0[first:first + 2 * P, g * SPAN:(g + 1) * SPAN].rearrange("(i p) f -> p i f", p=P)
            for i in range(2):
                nc.scalar.copy(out=y_rows[:, i, :].rearrange("p (m t) -> p m t", t=PACK),
                               in_=y_banks[u, 2 * pair + i][:].rearrange("p (t m) -> p m t", t=PACK))
                if fine:
                    nc.sync.dma_start(out=dst[:, i, :], in_=y_rows[:, i, :])
            if not fine:
                nc.sync.dma_start(out=dst, in_=y_rows[:])

        for c in range(PASSES):
            regroup_w(0, c, FIRST_GROUP_SPLIT)
        for first_slot in (0, 2):
            for c in range(PASSES):
                quantize_w(0, c, first_slot, 2)
        nc.vector.tensor_copy(out=vec_cols[:].bitcast(F32).rearrange("p (r i) -> p r i", i=2),
                              in_=vec_bank[:, :2 * P].rearrange("p (i r) -> p r i", i=2)[:, :2 * GROUPS, :])
        for c in range(PASSES):
            regroup_w(1, c)
        for c in range(PASSES):
            quantize_w(1, c)
        multiply(0)
        multiply(1)

        w_jobs = [(g, c) for g in range(2, GROUPS) for c in range(PASSES)]
        next_y = 0
        waiting = None
        for step in range(STEPS):
            u, pair = divmod(step, 2)
            activate(step)
            apply_gain(step)
            if waiting is not None:
                waiting[0](*waiting[1])
                waiting = None
            rest = pair == 1 and u <= len(w_jobs) and u % REST_EVERY == 0
            if pair == 0 and 1 <= u <= len(w_jobs):
                regroup_w(*w_jobs[u - 1])
                waiting = (quantize_w, w_jobs[u - 1])
            elif not rest and step not in (0, STEPS - 2):
                regroup_y(next_y)
                waiting = (quantize_y, (next_y,))
                next_y = next_y + 1
            if step >= 2:
                turn(step - 2)
            if step + 2 < STEPS:
                multiply(step + 2)
            if STORE_LAG <= step < STEPS - 1:
                store_y(step - STORE_LAG)
            if step >= STEPS - 2:
                store_y(step - STORE_LAG + 1)
            store_planes()

        assert next_y == UNITS - 1
        regroup_y(UNITS - 1)
        quantize_y(UNITS - 2)
        quantize_y(UNITS - 1)
        for step in (STEPS - 2, STEPS - 1):
            turn(step)
        for step in (STEPS - 2, STEPS - 1):
            store_y(step)
        store_planes()
